import numpy as np
import ml_dtypes


def mxq(x, axis, fmt="e4m3"):
    dtype, down = {"e4m3": (ml_dtypes.float8_e4m3fn, 7), "e5m2": (ml_dtypes.float8_e5m2, 14)}[fmt]
    v = np.moveaxis(np.asarray(x, np.float32).astype(ml_dtypes.bfloat16).astype(np.float64), axis, -1)
    blocks = v.reshape(v.shape[:-1] + (-1, 32))
    amax = np.abs(blocks).max(-1, keepdims=True)
    byte = np.maximum(np.where(amax > 0, np.frexp(amax)[1] - 1 + 127, 0) - down, 1)
    scale = np.exp2(byte - 127.0)
    codes = (blocks / scale).astype(np.float32).astype(dtype).astype(np.float64)
    return np.moveaxis((codes * scale).reshape(v.shape), -1, axis)


WIDE = False


def mx_kscale(k):
    if not WIDE:
        return np.ones(k)
    levels = np.array([10, -10, 5, -5, 0])
    if k % 512:
        return np.exp2(np.random.permutation(np.resize(levels, k // 32))).repeat(32)
    a = np.empty((k // 512, 16))
    for p in range(k // 512):
        a[p, :8] = np.random.permutation(np.resize(levels, 8))
        for g in range(8):
            far = levels[np.abs(levels - a[p, g]) >= 10]
            a[p, g + 8] = far[np.random.randint(len(far))]
    return np.exp2(a.ravel()).repeat(32)


def f64(x):
    return np.asarray(x).astype(np.float64)


def striped(idx):
    return np.tile(idx.reshape(-1, 16).T, (8, 1)).astype(np.uint16)


def unstriped(offs):
    return offs[:16].T.reshape(-1).astype(np.int64)


def pack_weight(w):
    k, n = w.shape
    w = f64(np.asarray(w, np.float32).astype(ml_dtypes.bfloat16)).reshape(k // 32, 32, n)
    amax = np.abs(w).max(1)
    byte = np.clip(np.where(amax > 0, np.frexp(amax)[1] - 1 + 127 - 7, 1), 1, 254)
    scaled = (w * np.exp2(127.0 - byte)[:, None, :]).reshape(k, n).astype(np.float32)
    words = np.ascontiguousarray(scaled.reshape(k // 512, 128, 4, n).transpose(0, 1, 3, 2)).astype(ml_dtypes.float8_e4m3fn).view(np.uint8)
    return words, np.ascontiguousarray(byte.astype(np.uint8).reshape(k // 512, 16, n))


def unpack_weight(words, scales):
    g, p, n, _ = words.shape
    vals = np.ascontiguousarray(words).view(ml_dtypes.float8_e4m3fn).astype(np.float64) * np.repeat(np.exp2(scales.astype(np.float64) - 127.0), 8, axis=1)[..., None]
    return vals.transpose(0, 1, 3, 2).reshape(g * 512, n)


K, T, S, D, N = 512, 2048, 1024, 4, 128


def setup_inputs():
    n = np.random.standard_normal
    s = mx_kscale(K)[:, None]
    packed_xT = pack_weight(n((K, T)) * s)
    packed_eT = pack_weight(n((K, T)) * s)
    return {
        "x_words": packed_xT[0],
        "x_scales": packed_xT[1],
        "e_words": packed_eT[0],
        "e_scales": packed_eT[1],
        "w1": (n((K, N)) / np.sqrt(2 * K) / s).astype(np.float32),
        "w2": (n((K, N)) / np.sqrt(2 * K) / s).astype(np.float32),
        "rec": (-n((N, 1))).astype(np.float32),
        "prec": (-np.random.uniform(0.3, 1.0, (N, 1))).astype(np.float32),
        "msg": (n((N, T)) * 0.7).astype(np.float32),
        "offs": striped(np.random.permutation(T)[:S]),
        "two": striped(np.random.permutation(T)[:S]),
    }


def reference(x_words, x_scales, e_words, e_scales, w1, w2, rec, prec, msg, offs, two):
    xq = unpack_weight(x_words, x_scales)[:, unstriped(offs)]
    e_two = unpack_weight(e_words, e_scales)[:, unstriped(two)]
    y = mxq(f64(w1), 0, "e4m3").T @ xq + mxq(f64(w2), 0, "e4m3").T @ e_two
    df = y + f64(rec)
    mt = f64(prec) * ((df) ** 2) + f64(msg)[:, unstriped(two)]
    return mt.reshape(len(mt), -1, D).max(axis=2)

@@ -1,0 +1,142 @@
+from contextlib import ExitStack
+
+import concourse.mybir as mybir
+
+K, T, S, D, N = 512, 2048, 1024, 4, 128
+FLOPS = 2 * 2 * K * N * S
+
+F32 = mybir.dt.float32
+BF16 = mybir.dt.bfloat16
+I32 = mybir.dt.int32
+U32 = mybir.dt.uint32
+U16 = mybir.dt.uint16
+U8 = mybir.dt.uint8
+FP8X4 = mybir.dt.float8_e4m3fn_x4
+ACT = mybir.ActivationFunctionType
+ALU = mybir.AluOpType
+
+P = 128
+PACK = 4
+LANES = 16
+PRODUCT_COLS = 256
+MSG_PIECES = (256, 256, 256, 128, 128)
+STORE_AFTER = (768, 1024)
+
+
+def tile_picked_yscma_max_p_kernel(
+    tc, x_words, x_scales, e_words, e_scales, w1, w2, rec, prec, msg, offs, two, out
+):
+    nc = tc.nc
+    with ExitStack() as ctx:
+        keep = ctx.enter_context(tc.tile_pool(name="keep", bufs=1))
+        psum = ctx.enter_context(tc.psum_pool(name="psum", bufs=1))
+
+        offs_sb = keep.tile([P, S // LANES], U16, name="offs_sb")
+        two_sb = keep.tile([P, S // LANES], U16, name="two_sb")
+        rec_sb = keep.tile([P, 1], F32, name="rec_sb")
+        prec_sb = keep.tile([P, 1], F32, name="prec_sb")
+        x_scale_table = keep.tile([P, T], U8, name="x_scale_table", align_bytes=64)
+        e_scale_table = keep.tile([P, T], U8, name="e_scale_table", align_bytes=64)
+        x_word_table = keep.tile([P, T], I32, name="x_word_table", align_bytes=64)
+        e_word_table = keep.tile([P, T], I32, name="e_word_table", align_bytes=64)
+        msg_table = keep.tile([P, T], F32, name="msg_table", align_bytes=64)
+        w_raw = [keep.tile([P, PACK, N], F32, name="w_raw%d" % i) for i in range(2)]
+
+        def load_scales(eng, table, scales):
+            for q in range(4):
+                eng.dma_start(
+                    table[32 * q : 32 * q + 4, :].bitcast(I32),
+                    scales[0, 4 * q : 4 * q + 4, :].bitcast(I32),
+                )
+
+        def load_words(eng, table, words):
+            eng.dma_start(table[:], words[0].rearrange("p n t -> p (n t)").bitcast(I32))
+
+        def load_w(eng, i, w):
+            eng.dma_start(w_raw[i][:], w.rearrange("(p j) n -> p j n", j=PACK))
+
+        nc.vector.memset(x_scale_table[:].bitcast(I32), 0)
+        nc.vector.memset(e_scale_table[:].bitcast(I32), 0)
+        nc.sync.dma_start(offs_sb[:], offs)
+        nc.sync.dma_start(two_sb[:], two)
+        nc.sync.dma_start(rec_sb[:], rec)
+        nc.sync.dma_start(prec_sb[:], prec)
+        load_scales(nc.sync, x_scale_table, x_scales)
+        load_scales(nc.sync, e_scale_table, e_scales)
+        load_words(nc.sync, x_word_table, x_words)
+        load_w(nc.sync, 0, w1)
+        load_w(nc.sync, 1, w2)
+        load_words(nc.sync, e_word_table, e_words)
+        nc.sync.dma_start(msg_table[:], msg)
+
+        x_scale = keep.tile([P, S], U8, name="x_scale", align_bytes=64)
+        e_scale = keep.tile([P, S], U8, name="e_scale", align_bytes=64)
+        x_word = keep.tile([P, S], U32, name="x_word", align_bytes=64)
+        e_word = keep.tile([P, S], U32, name="e_word", align_bytes=64)
+        w_grouped = keep.tile([P, 2, N, PACK], BF16, name="w_grouped", align_bytes=64)
+        w_word = keep.tile([P, 2 * N], U32, name="w_word", align_bytes=64)
+        w_scale = keep.tile([P, 2 * N], U8, name="w_scale", align_bytes=64)
+        square = keep.tile([P, S], F32, name="square", align_bytes=64)
+        term = keep.tile([P, S], F32, name="term", align_bytes=64)
+        metric = keep.tile([P, S], F32, name="metric", align_bytes=64)
+        best = keep.tile([P, S // D], F32, name="best", align_bytes=64)
+
+        for i in range(2):
+            nc.scalar.activation(w_grouped[:, i, :, :], w_raw[i][:].rearrange("p j n -> p n j"), ACT.Copy)
+
+        nc.vector.tensor_copy(x_scale[:], x_scale_table[:].indirect(offs_sb[:]))
+        nc.vector.tensor_copy(e_scale[:], e_scale_table[:].indirect(two_sb[:]))
+        nc.vector.tensor_copy(x_word[:], x_word_table[:].bitcast(U32).indirect(offs_sb[:]))
+        nc.vector.quantize_mx(
+            out=w_word[:].bitcast(FP8X4),
+            scales=w_scale[:],
+            in_=w_grouped[:].rearrange("p i n j -> p (i n j)"),
+        )
+
+        for c0 in range(0, S, PRODUCT_COLS):
+            cols = slice(c0, c0 + PRODUCT_COLS)
+            nc.vector.tensor_copy(
+                e_word[:, cols],
+                e_word_table[:].bitcast(U32).indirect(two_sb[:, c0 // LANES : (c0 + PRODUCT_COLS) // LANES]),
+            )
+            y = psum.tile([P, PRODUCT_COLS], F32, name="y%d" % c0)
+            for i, (word, scale) in enumerate(((x_word, x_scale), (e_word, e_scale))):
+                nc.tensor.matmul_mx(
+                    out=y[:],
+                    lhsT=w_word[:, i * N : (i + 1) * N].bitcast(FP8X4),
+                    lhsT_scale=w_scale[:, i * N : (i + 1) * N],
+                    rhs=word[:, cols].bitcast(FP8X4),
+                    rhs_scale=scale[:, cols],
+                    start=(i == 0),
+                    stop=(i == 1),
+                )
+            nc.scalar.activation(square[:, cols], y[:], ACT.Square, bias=rec_sb[:])
+            nc.scalar.activation(term[:, cols], square[:, cols], ACT.Copy, scale=prec_sb[:])
+
+        c0, stored, pending = 0, 0, None
+
+        def finish(a, b, stored):
+            nc.vector.tensor_reduce(
+                best[:, a // D : b // D],
+                metric[:, a:b].rearrange("p (v d) -> p v d", d=D),
+                mybir.AxisListType.X,
+                ALU.max,
+            )
+            if b in STORE_AFTER:
+                nc.sync.dma_start(out[:, stored // D : b // D], best[:, stored // D : b // D])
+                return b
+            return stored
+
+        for width in MSG_PIECES:
+            cols = slice(c0, c0 + width)
+            nc.vector.tensor_tensor(
+                metric[:, cols],
+                msg_table[:].indirect(two_sb[:, c0 // LANES : (c0 + width) // LANES]),
+                term[:, cols],
+                ALU.add,
+            )
+            if pending is not None:
+                stored = finish(pending[0], pending[1], stored)
+            pending = (c0, c0 + width)
+            c0 = c0 + width
+        finish(pending[0], pending[1], stored)

@@ -19,7 +19,7 @@ P = 128
 PACK = 4
 LANES = 16
 PRODUCT_COLS = 256
-MSG_PIECES = (256, 256, 256, 128, 128)
+MSG_PIECES = (256, 256, 256, 256)
 STORE_AFTER = (768, 1024)
 
 
@@ -59,13 +59,13 @@ def tile_picked_yscma_max_p_kernel(
         nc.vector.memset(e_scale_table[:].bitcast(I32), 0)
         nc.sync.dma_start(offs_sb[:], offs)
         nc.sync.dma_start(two_sb[:], two)
-        nc.sync.dma_start(rec_sb[:], rec)
-        nc.sync.dma_start(prec_sb[:], prec)
         load_scales(nc.sync, x_scale_table, x_scales)
         load_scales(nc.sync, e_scale_table, e_scales)
         load_words(nc.sync, x_word_table, x_words)
         load_w(nc.sync, 0, w1)
         load_w(nc.sync, 1, w2)
+        nc.sync.dma_start(rec_sb[:], rec)
+        nc.sync.dma_start(prec_sb[:], prec)
         load_words(nc.sync, e_word_table, e_words)
         nc.sync.dma_start(msg_table[:], msg)
 

@@ -76,7 +76,6 @@ def tile_picked_yscma_max_p_kernel(
         w_grouped = keep.tile([P, 2, N, PACK], BF16, name="w_grouped", align_bytes=64)
         w_word = keep.tile([P, 2 * N], U32, name="w_word", align_bytes=64)
         w_scale = keep.tile([P, 2 * N], U8, name="w_scale", align_bytes=64)
-        square = keep.tile([P, S], F32, name="square", align_bytes=64)
         term = keep.tile([P, S], F32, name="term", align_bytes=64)
         metric = keep.tile([P, S], F32, name="metric", align_bytes=64)
         best = keep.tile([P, S // D], F32, name="best", align_bytes=64)
@@ -110,8 +109,9 @@ def tile_picked_yscma_max_p_kernel(
                     start=(i == 0),
                     stop=(i == 1),
                 )
-            nc.scalar.activation(square[:, cols], y[:], ACT.Square, bias=rec_sb[:])
-            nc.scalar.activation(term[:, cols], square[:, cols], ACT.Copy, scale=prec_sb[:])
+            square = keep.tile([P, PRODUCT_COLS], F32, name="square", bufs=2, align_bytes=64)
+            nc.scalar.activation(square[:], y[:], ACT.Square, bias=rec_sb[:])
+            nc.scalar.activation(term[:, cols], square[:], ACT.Copy, scale=prec_sb[:])
 
         c0, stored, pending = 0, 0, None
 

from contextlib import ExitStack

import concourse.mybir as mybir

K, T, S, D, N = 512, 2048, 1024, 4, 128
FLOPS = 2 * 2 * K * N * S

F32 = mybir.dt.float32
BF16 = mybir.dt.bfloat16
I32 = mybir.dt.int32
U32 = mybir.dt.uint32
U16 = mybir.dt.uint16
U8 = mybir.dt.uint8
FP8X4 = mybir.dt.float8_e4m3fn_x4
ACT = mybir.ActivationFunctionType
ALU = mybir.AluOpType

P = 128
PACK = 4
LANES = 16
PRODUCT_COLS = 256
MSG_PIECES = (256, 256, 256, 256)
STORE_AFTER = (768, 1024)


def tile_picked_yscma_max_p_kernel(
    tc, x_words, x_scales, e_words, e_scales, w1, w2, rec, prec, msg, offs, two, out
):
    nc = tc.nc
    with ExitStack() as ctx:
        keep = ctx.enter_context(tc.tile_pool(name="keep", bufs=1))
        psum = ctx.enter_context(tc.psum_pool(name="psum", bufs=1))

        offs_sb = keep.tile([P, S // LANES], U16, name="offs_sb")
        two_sb = keep.tile([P, S // LANES], U16, name="two_sb")
        rec_sb = keep.tile([P, 1], F32, name="rec_sb")
        prec_sb = keep.tile([P, 1], F32, name="prec_sb")
        x_scale_table = keep.tile([P, T], U8, name="x_scale_table", align_bytes=64)
        e_scale_table = keep.tile([P, T], U8, name="e_scale_table", align_bytes=64)
        x_word_table = keep.tile([P, T], I32, name="x_word_table", align_bytes=64)
        e_word_table = keep.tile([P, T], I32, name="e_word_table", align_bytes=64)
        msg_table = keep.tile([P, T], F32, name="msg_table", align_bytes=64)
        w_raw = [keep.tile([P, PACK, N], F32, name="w_raw%d" % i) for i in range(2)]

        def load_scales(eng, table, scales):
            for q in range(4):
                eng.dma_start(
                    table[32 * q : 32 * q + 4, :].bitcast(I32),
                    scales[0, 4 * q : 4 * q + 4, :].bitcast(I32),
                )

        def load_words(eng, table, words):
            eng.dma_start(table[:], words[0].rearrange("p n t -> p (n t)").bitcast(I32))

        def load_w(eng, i, w):
            eng.dma_start(w_raw[i][:], w.rearrange("(p j) n -> p j n", j=PACK))

        nc.vector.memset(x_scale_table[:].bitcast(I32), 0)
        nc.vector.memset(e_scale_table[:].bitcast(I32), 0)
        nc.sync.dma_start(offs_sb[:], offs)
        nc.sync.dma_start(two_sb[:], two)
        load_scales(nc.sync, x_scale_table, x_scales)
        load_scales(nc.sync, e_scale_table, e_scales)
        load_words(nc.sync, x_word_table, x_words)
        load_w(nc.sync, 0, w1)
        load_w(nc.sync, 1, w2)
        nc.sync.dma_start(rec_sb[:], rec)
        nc.sync.dma_start(prec_sb[:], prec)
        load_words(nc.sync, e_word_table, e_words)
        nc.sync.dma_start(msg_table[:], msg)

        x_scale = keep.tile([P, S], U8, name="x_scale", align_bytes=64)
        e_scale = keep.tile([P, S], U8, name="e_scale", align_bytes=64)
        x_word = keep.tile([P, S], U32, name="x_word", align_bytes=64)
        e_word = keep.tile([P, S], U32, name="e_word", align_bytes=64)
        w_grouped = keep.tile([P, 2, N, PACK], BF16, name="w_grouped", align_bytes=64)
        w_word = keep.tile([P, 2 * N], U32, name="w_word", align_bytes=64)
        w_scale = keep.tile([P, 2 * N], U8, name="w_scale", align_bytes=64)
        term = keep.tile([P, S], F32, name="term", align_bytes=64)
        metric = keep.tile([P, S], F32, name="metric", align_bytes=64)
        best = keep.tile([P, S // D], F32, name="best", align_bytes=64)

        for i in range(2):
            nc.scalar.activation(w_grouped[:, i, :, :], w_raw[i][:].rearrange("p j n -> p n j"), ACT.Copy)

        nc.vector.tensor_copy(x_scale[:], x_scale_table[:].indirect(offs_sb[:]))
        nc.vector.tensor_copy(e_scale[:], e_scale_table[:].indirect(two_sb[:]))
        nc.vector.tensor_copy(x_word[:], x_word_table[:].bitcast(U32).indirect(offs_sb[:]))
        nc.vector.quantize_mx(
            out=w_word[:].bitcast(FP8X4),
            scales=w_scale[:],
            in_=w_grouped[:].rearrange("p i n j -> p (i n j)"),
        )

        for c0 in range(0, S, PRODUCT_COLS):
            cols = slice(c0, c0 + PRODUCT_COLS)
            nc.vector.tensor_copy(
                e_word[:, cols],
                e_word_table[:].bitcast(U32).indirect(two_sb[:, c0 // LANES : (c0 + PRODUCT_COLS) // LANES]),
            )
            y = psum.tile([P, PRODUCT_COLS], F32, name="y%d" % c0)
            for i, (word, scale) in enumerate(((x_word, x_scale), (e_word, e_scale))):
                nc.tensor.matmul_mx(
                    out=y[:],
                    lhsT=w_word[:, i * N : (i + 1) * N].bitcast(FP8X4),
                    lhsT_scale=w_scale[:, i * N : (i + 1) * N],
                    rhs=word[:, cols].bitcast(FP8X4),
                    rhs_scale=scale[:, cols],
                    start=(i == 0),
                    stop=(i == 1),
                )
            square = keep.tile([P, PRODUCT_COLS], F32, name="square", bufs=2, align_bytes=64)
            nc.scalar.activation(square[:], y[:], ACT.Square, bias=rec_sb[:])
            nc.scalar.activation(term[:, cols], square[:], ACT.Copy, scale=prec_sb[:])

        c0, stored, pending = 0, 0, None

        def finish(a, b, stored):
            nc.vector.tensor_reduce(
                best[:, a // D : b // D],
                metric[:, a:b].rearrange("p (v d) -> p v d", d=D),
                mybir.AxisListType.X,
                ALU.max,
            )
            if b in STORE_AFTER:
                nc.sync.dma_start(out[:, stored // D : b // D], best[:, stored // D : b // D])
                return b
            return stored

        for width in MSG_PIECES:
            cols = slice(c0, c0 + width)
            nc.vector.tensor_tensor(
                metric[:, cols],
                msg_table[:].indirect(two_sb[:, c0 // LANES : (c0 + width) // LANES]),
                term[:, cols],
                ALU.add,
            )
            if pending is not None:
                stored = finish(pending[0], pending[1], stored)
            pending = (c0, c0 + width)
            c0 = c0 + width
        finish(pending[0], pending[1], stored)
